import numpy as np
import ml_dtypes


def mxq(x, axis, fmt="e4m3"):
    dtype, down = {"e4m3": (ml_dtypes.float8_e4m3fn, 7), "e5m2": (ml_dtypes.float8_e5m2, 14)}[fmt]
    v = np.moveaxis(np.asarray(x, np.float32).astype(ml_dtypes.bfloat16).astype(np.float64), axis, -1)
    blocks = v.reshape(v.shape[:-1] + (-1, 32))
    amax = np.abs(blocks).max(-1, keepdims=True)
    byte = np.maximum(np.where(amax > 0, np.frexp(amax)[1] - 1 + 127, 0) - down, 1)
    scale = np.exp2(byte - 127.0)
    codes = (blocks / scale).astype(np.float32).astype(dtype).astype(np.float64)
    return np.moveaxis((codes * scale).reshape(v.shape), -1, axis)


WIDE = False


def mx_kscale(k):
    if not WIDE:
        return np.ones(k)
    levels = np.array([10, -10, 5, -5, 0])
    if k % 512:
        return np.exp2(np.random.permutation(np.resize(levels, k // 32))).repeat(32)
    a = np.empty((k // 512, 16))
    for p in range(k // 512):
        a[p, :8] = np.random.permutation(np.resize(levels, 8))
        for g in range(8):
            far = levels[np.abs(levels - a[p, g]) >= 10]
            a[p, g + 8] = far[np.random.randint(len(far))]
    return np.exp2(a.ravel()).repeat(32)


def f64(x):
    return np.asarray(x).astype(np.float64)


def striped(idx):
    return np.tile(idx.reshape(-1, 16).T, (8, 1)).astype(np.uint16)


def unstriped(offs):
    return offs[:16].T.reshape(-1).astype(np.int64)


E2M1 = np.array([0.0, 0.5, 1.0, 1.5, 2.0, 3.0, 4.0, 6.0, -0.0, -0.5, -1.0, -1.5, -2.0, -3.0, -4.0, -6.0])


def pack_weight(w, fmt):
    k, n = w.shape
    w = f64(np.asarray(w, np.float32).astype(ml_dtypes.bfloat16)).reshape(k // 32, 32, n)
    amax = np.abs(w).max(1)
    if fmt == "e4m3":
        byte = np.frexp(amax)[1] - 1 + 127 - 7
    else:
        mant, ex = np.frexp(amax / 6.0)
        byte = np.where(mant > 0.5, ex, ex - 1) + 127
    byte = np.clip(np.where(amax > 0, byte, 1), 1, 254)
    scaled = (w * np.exp2(127.0 - byte)[:, None, :]).reshape(k, n).astype(np.float32)
    by_word = np.ascontiguousarray(scaled.reshape(k // 512, 128, 4, n).transpose(0, 1, 3, 2))
    if fmt == "e4m3":
        words = by_word.astype(ml_dtypes.float8_e4m3fn).view(np.uint8)
    else:
        c = by_word.astype(ml_dtypes.float4_e2m1fn).view(np.uint8) & 0xF
        words = (c[..., 0::2] | (c[..., 1::2] << 4)).reshape(k // 512, 128, 2 * n)
    return np.ascontiguousarray(words), np.ascontiguousarray(byte.astype(np.uint8).reshape(k // 512, 16, n))


def unpack_weight(words, scales, fmt):
    g, _, n = scales.shape
    words = np.ascontiguousarray(words).reshape(g, 128, n, -1)
    if fmt == "e4m3":
        vals = words.view(ml_dtypes.float8_e4m3fn).astype(np.float64)
    else:
        nib = np.empty((g, 128, n, 4), np.uint8)
        nib[..., 0::2] = words & 0xF
        nib[..., 1::2] = words >> 4
        vals = E2M1[nib]
    vals = vals * np.repeat(np.exp2(scales.astype(np.float64) - 127.0), 8, axis=1)[..., None]
    return vals.transpose(0, 1, 3, 2).reshape(g * 512, n)


def pack_table(v):
    words, scales = pack_weight(v, "e4m3")
    return np.concatenate([words.reshape(words.shape[0], -1), scales.reshape(scales.shape[0], -1)], axis=1)


def unpack_table(tab):
    g, t = tab.shape[0], tab.shape[1] // 528
    return unpack_weight(tab[:, :512 * t].reshape(g, 128, t, 4), tab[:, 512 * t:].reshape(g, 16, t), "e4m3")


G, K, M, T, S = 2, 1024, 256, 2048, 512


def setup_inputs():
    n = np.random.standard_normal
    s = mx_kscale(K)[:, None]
    p_w4 = pack_weight(n((K, M)) / np.sqrt(K) / s, "e2m1")
    return {
        "tab": pack_table(n((K, T)) * s),
        "w4_words": p_w4[0],
        "w4_scales": p_w4[1],
        "dw": (0.3 * n((K, M)) / np.sqrt(K) / s).astype(np.float32),
        "b": (0.3 * n(256)).astype(np.float32),
        "offs": striped(np.concatenate([np.random.permutation(T)[:S] for _ in range(G)])),
    }


def reference(tab, w4_words, w4_scales, dw, b, offs):
    tab_ = unpack_table(tab)[:, unstriped(offs).reshape(G, S)].sum(1)
    w4_ = unpack_weight(w4_words, w4_scales, "e2m1")
    dw_ = mxq(f64(dw), 0, "e4m3")
    y = tab_.T @ w4_ + tab_.T @ dw_
    return y + f64(b)[None, :]

@@ -1,0 +1,129 @@
+from contextlib import ExitStack
+
+import concourse.mybir as mybir
+from concourse.masks import make_identity
+
+G, K, M, T, S = 2, 1024, 256, 2048, 512
+FLOPS = 2 * 2 * G * K * M * S
+
+F32 = mybir.dt.float32
+BF16 = mybir.dt.bfloat16
+I32 = mybir.dt.int32
+U32 = mybir.dt.uint32
+U16 = mybir.dt.uint16
+U8 = mybir.dt.uint8
+FP8X4 = mybir.dt.float8_e4m3fn_x4
+FP4X4 = mybir.dt.float4_e2m1fn_x4
+ADD = mybir.AluOpType.add
+
+P = 128
+PASSES = K // 512
+HALF = 256
+TILES = S // P
+
+
+def tile_list_tabbag_tm_sum_bias_kernel(tc, tab, w4_words, w4_scales, dw, b, offs, out):
+    nc = tc.nc
+    with ExitStack() as ctx:
+        lists = ctx.enter_context(tc.tile_pool(name="lists", bufs=1))
+        keep = ctx.enter_context(tc.tile_pool(name="keep", bufs=1))
+        psum = ctx.enter_context(tc.psum_pool(name="psum", bufs=1))
+
+        offsets = lists.tile([P, G * S // 16], U16, name="offsets")
+        nc.sync.dma_start(offsets[:], offs)
+
+        tab32 = tab.bitcast(I32)
+        scale_win = keep.tile([P, T], U8, name="scale_win", align_bytes=64)
+        nc.gpsimd.memset(scale_win[:].bitcast(I32), 0)
+        w4w = keep.tile([P, PASSES, 2 * M], U8, name="w4w", align_bytes=64)
+        nc.sync.dma_start(w4w[:].bitcast(I32), w4_words.bitcast(I32).rearrange("a p w -> p a w"))
+        rows0 = tab32[0, P * T :].rearrange("(q r w) -> r q w", q=4, r=4)
+        for r in range(4):
+            nc.sync.dma_start(scale_win[r:P:32, :].bitcast(I32), rows0[r])
+        rows1 = tab32[1, P * T :].rearrange("(q w) -> q w", q=16)
+        nc.sync.dma_start(scale_win[4:P:8, :].bitcast(I32), rows1)
+
+        w4s = keep.tile([P, PASSES, M], U8, name="w4s", align_bytes=64)
+        nc.vector.memset(w4s[:].rearrange("p a n -> p (a n)").bitcast(I32), 0)
+        plane1 = keep.tile([P, G * S], U8, name="plane1", align_bytes=64)
+        nc.vector.memset(plane1[:].bitcast(I32), 0)
+
+        words = [keep.tile([P, T], U32, name="words%d" % a, align_bytes=64) for a in range(PASSES)]
+        nc.sync.dma_start(words[0][:].bitcast(I32), tab32[0, : P * T].rearrange("(p t) -> p t", p=P))
+        w4rows = w4_scales.bitcast(I32).rearrange("a (q r) w -> r q a w", r=4)
+        for r in range(4):
+            nc.sync.dma_start(w4s[r:P:32, :, :].bitcast(I32), w4rows[r])
+        nc.sync.dma_start(words[1][:].bitcast(I32), tab32[1, : P * T].rearrange("(p t) -> p t", p=P))
+        raw = [keep.tile([P, 4, M], F32, name="raw%d" % a) for a in range(PASSES)]
+        for a in range(PASSES):
+            nc.sync.dma_start(raw[a][:], dw[512 * a : 512 * (a + 1), :].rearrange("(p j) n -> p j n", j=4))
+
+        b_col = keep.tile([P, 2], F32, name="b_col")
+        nc.gpsimd.dma_start(b_col[:], b.rearrange("(p j) -> p j", j=2))
+        ident = keep.tile([P, P], F32, name="ident")
+        nc.vector.memset(ident[:], 0.0)
+        make_identity(nc, ident[:], nomemset=True)
+        bias_ps = psum.tile([P, 2, P], F32, name="bias_ps")
+        for j in range(2):
+            nc.tensor.transpose(bias_ps[:, j, :], b_col[:, j : j + 1].to_broadcast([P, P]), ident[:])
+        bias = keep.tile([P, P, 2], F32, name="bias")
+        nc.scalar.copy(bias[:], bias_ps[:].rearrange("m j p -> m p j"))
+
+        picked_scales = keep.tile([P, G * S], U8, name="picked_scales", align_bytes=64)
+        nc.vector.tensor_copy(picked_scales[:], scale_win[:].indirect(offsets[:]))
+        for r in range(4):
+            nc.scalar.dma_start(plane1[r:P:32, :].bitcast(I32), picked_scales[8 * r + 4 : P : 32, :].bitcast(I32))
+        planes = [picked_scales, plane1]
+
+        acc = [psum.tile([P, M], F32, name="acc%d" % t) for t in range(TILES)]
+        picked = {}
+        for a in range(PASSES):
+            for h in range(S // HALF):
+                for g in range(G):
+                    m0 = g * S + h * HALF
+                    pk = keep.tile([P, HALF], U32, name="pk%d%d%d" % (a, h, g), align_bytes=64)
+                    nc.vector.tensor_copy(pk[:], words[a][:].indirect(offsets[:, m0 // 16 : (m0 + HALF) // 16]))
+                    picked[a, h, g] = pk
+                    for u in range(HALF // P):
+                        t = h * (HALF // P) + u
+                        for c in range(M // P):
+                            nc.tensor.matmul_mx(
+                                out=acc[t][:, c * P : (c + 1) * P],
+                                lhsT=pk[:, u * P : (u + 1) * P].bitcast(FP8X4),
+                                lhsT_scale=planes[a][:, m0 + u * P : m0 + (u + 1) * P],
+                                rhs=w4w[:, a, 2 * c * P : 2 * (c + 1) * P].bitcast(FP4X4),
+                                rhs_scale=w4s[:, a, c * P : (c + 1) * P],
+                                start=(a == 0 and g == 0 and c == 0),
+                                stop=False,
+                            )
+
+        SPLIT = 160
+        for a in range(PASSES):
+            grouped = keep.tile([P, M, 4], BF16, name="grouped%d" % a, align_bytes=64)
+            src = raw[a][:].rearrange("p j n -> p n j")
+            if a == 0:
+                nc.scalar.copy(grouped[:], src)
+            else:
+                nc.vector.tensor_copy(grouped[:, :SPLIT, :], src[:, :SPLIT, :])
+                nc.scalar.copy(grouped[:, SPLIT:, :], src[:, SPLIT:, :])
+            codes = keep.tile([P, M], U32, name="codes%d" % a, align_bytes=64)
+            scales = keep.tile([P, M], U8, name="scales%d" % a, align_bytes=64)
+            nc.vector.quantize_mx(out=codes[:].bitcast(FP8X4), scales=scales[:], in_=grouped[:].rearrange("p n j -> p (n j)"))
+            for t in range(TILES):
+                h, u = divmod(t, HALF // P)
+                for g in range(G):
+                    m0 = g * S + t * P
+                    nc.tensor.matmul_mx(
+                        out=acc[t][:],
+                        lhsT=picked[a, h, g][:, u * P : (u + 1) * P].bitcast(FP8X4),
+                        lhsT_scale=planes[a][:, m0 : m0 + P],
+                        rhs=codes[:].bitcast(FP8X4),
+                        rhs_scale=scales[:],
+                        start=False,
+                        stop=(a == PASSES - 1 and g == G - 1),
+                    )
+
+        for t in range(TILES):
+            res = keep.tile([P, M], F32, name="res%d" % t)
+            nc.vector.tensor_tensor(res[:], acc[t][:], bias[:].rearrange("m p j -> m (p j)"), ADD)
+            nc.sync.dma_start(out[t * P : (t + 1) * P, :], res[:])

@@ -35,33 +35,30 @@ def tile_list_tabbag_tm_sum_bias_kernel(tc, tab, w4_words, w4_scales, dw, b, off
         tab32 = tab.bitcast(I32)
         scale_win = keep.tile([P, T], U8, name="scale_win", align_bytes=64)
         nc.gpsimd.memset(scale_win[:].bitcast(I32), 0)
-        w4w = keep.tile([P, PASSES, 2 * M], U8, name="w4w", align_bytes=64)
-        nc.sync.dma_start(w4w[:].bitcast(I32), w4_words.bitcast(I32).rearrange("a p w -> p a w"))
-        rows0 = tab32[0, P * T :].rearrange("(q r w) -> r q w", q=4, r=4)
-        for r in range(4):
-            nc.sync.dma_start(scale_win[r:P:32, :].bitcast(I32), rows0[r])
-        rows1 = tab32[1, P * T :].rearrange("(q w) -> q w", q=16)
-        nc.sync.dma_start(scale_win[4:P:8, :].bitcast(I32), rows1)
-
+        ident = keep.tile([P, P], F32, name="ident")
+        nc.vector.memset(ident[:], 0.0)
         w4s = keep.tile([P, PASSES, M], U8, name="w4s", align_bytes=64)
         nc.vector.memset(w4s[:].rearrange("p a n -> p (a n)").bitcast(I32), 0)
         plane1 = keep.tile([P, G * S], U8, name="plane1", align_bytes=64)
         nc.vector.memset(plane1[:].bitcast(I32), 0)
 
         words = [keep.tile([P, T], U32, name="words%d" % a, align_bytes=64) for a in range(PASSES)]
-        nc.sync.dma_start(words[0][:].bitcast(I32), tab32[0, : P * T].rearrange("(p t) -> p t", p=P))
+        raw = [keep.tile([P, 4, M], F32, name="raw%d" % a) for a in range(PASSES)]
+        b_col = keep.tile([P, 2], F32, name="b_col")
+        nc.sync.dma_start(b_col[:], b.rearrange("(p j) -> p j", j=2))
+        nc.sync.dma_start(raw[0][:], dw[0:512, :].rearrange("(p j) n -> p j n", j=4))
+        rows = tab32[:, P * T :].rearrange("a (q r w) -> r q a w", q=4, r=4)
+        for r in range(4):
+            nc.sync.dma_start(scale_win[r:P:16, :].bitcast(I32), rows[r])
+        for a in range(PASSES):
+            nc.sync.dma_start(words[a][:].bitcast(I32), tab32[a, : P * T].rearrange("(p t) -> p t", p=P))
+        w4w = keep.tile([P, PASSES, 2 * M], U8, name="w4w", align_bytes=64)
+        nc.sync.dma_start(w4w[:].bitcast(I32), w4_words.bitcast(I32).rearrange("a p w -> p a w"))
         w4rows = w4_scales.bitcast(I32).rearrange("a (q r) w -> r q a w", r=4)
         for r in range(4):
             nc.sync.dma_start(w4s[r:P:32, :, :].bitcast(I32), w4rows[r])
-        nc.sync.dma_start(words[1][:].bitcast(I32), tab32[1, : P * T].rearrange("(p t) -> p t", p=P))
-        raw = [keep.tile([P, 4, M], F32, name="raw%d" % a) for a in range(PASSES)]
-        for a in range(PASSES):
-            nc.sync.dma_start(raw[a][:], dw[512 * a : 512 * (a + 1), :].rearrange("(p j) n -> p j n", j=4))
+        nc.sync.dma_start(raw[1][:], dw[512:1024, :].rearrange("(p j) n -> p j n", j=4))
 
-        b_col = keep.tile([P, 2], F32, name="b_col")
-        nc.gpsimd.dma_start(b_col[:], b.rearrange("(p j) -> p j", j=2))
-        ident = keep.tile([P, P], F32, name="ident")
-        nc.vector.memset(ident[:], 0.0)
         make_identity(nc, ident[:], nomemset=True)
         bias_ps = psum.tile([P, 2, P], F32, name="bias_ps")
         for j in range(2):
@@ -71,57 +68,75 @@ def tile_list_tabbag_tm_sum_bias_kernel(tc, tab, w4_words, w4_scales, dw, b, off
 
         picked_scales = keep.tile([P, G * S], U8, name="picked_scales", align_bytes=64)
         nc.vector.tensor_copy(picked_scales[:], scale_win[:].indirect(offsets[:]))
-        for r in range(4):
-            nc.scalar.dma_start(plane1[r:P:32, :].bitcast(I32), picked_scales[8 * r + 4 : P : 32, :].bitcast(I32))
+        nc.scalar.dma_start(plane1[0:100, :].bitcast(I32), picked_scales[16:116, :].bitcast(I32))
         planes = [picked_scales, plane1]
 
         acc = [psum.tile([P, M], F32, name="acc%d" % t) for t in range(TILES)]
         picked = {}
-        for a in range(PASSES):
-            for h in range(S // HALF):
-                for g in range(G):
-                    m0 = g * S + h * HALF
-                    pk = keep.tile([P, HALF], U32, name="pk%d%d%d" % (a, h, g), align_bytes=64)
-                    nc.vector.tensor_copy(pk[:], words[a][:].indirect(offsets[:, m0 // 16 : (m0 + HALF) // 16]))
-                    picked[a, h, g] = pk
-                    for u in range(HALF // P):
-                        t = h * (HALF // P) + u
-                        for c in range(M // P):
-                            nc.tensor.matmul_mx(
-                                out=acc[t][:, c * P : (c + 1) * P],
-                                lhsT=pk[:, u * P : (u + 1) * P].bitcast(FP8X4),
-                                lhsT_scale=planes[a][:, m0 + u * P : m0 + (u + 1) * P],
-                                rhs=w4w[:, a, 2 * c * P : 2 * (c + 1) * P].bitcast(FP4X4),
-                                rhs_scale=w4s[:, a, c * P : (c + 1) * P],
-                                start=(a == 0 and g == 0 and c == 0),
-                                stop=False,
-                            )
+        quantised = {}
 
-        SPLIT = 160
-        for a in range(PASSES):
+        def quantise(a):
             grouped = keep.tile([P, M, 4], BF16, name="grouped%d" % a, align_bytes=64)
-            src = raw[a][:].rearrange("p j n -> p n j")
-            if a == 0:
-                nc.scalar.copy(grouped[:], src)
-            else:
-                nc.vector.tensor_copy(grouped[:, :SPLIT, :], src[:, :SPLIT, :])
-                nc.scalar.copy(grouped[:, SPLIT:, :], src[:, SPLIT:, :])
+            nc.scalar.copy(
+                grouped[:].rearrange("p (c i) j -> p c j i", i=4),
+                raw[a][:].rearrange("p j (c i) -> p c j i", i=4),
+            )
             codes = keep.tile([P, M], U32, name="codes%d" % a, align_bytes=64)
             scales = keep.tile([P, M], U8, name="scales%d" % a, align_bytes=64)
             nc.vector.quantize_mx(out=codes[:].bitcast(FP8X4), scales=scales[:], in_=grouped[:].rearrange("p n j -> p (n j)"))
-            for t in range(TILES):
-                h, u = divmod(t, HALF // P)
-                for g in range(G):
-                    m0 = g * S + t * P
-                    nc.tensor.matmul_mx(
-                        out=acc[t][:],
-                        lhsT=picked[a, h, g][:, u * P : (u + 1) * P].bitcast(FP8X4),
-                        lhsT_scale=planes[a][:, m0 : m0 + P],
-                        rhs=codes[:].bitcast(FP8X4),
-                        rhs_scale=scales[:],
-                        start=False,
-                        stop=(a == PASSES - 1 and g == G - 1),
-                    )
+            quantised[a] = (codes, scales)
+
+        def gather(a, h, g):
+            m0 = g * S + h * HALF
+            pk = keep.tile([P, HALF], U32, name="pk%d%d%d" % (a, h, g), align_bytes=64)
+            nc.vector.tensor_copy(pk[:], words[a][:].indirect(offsets[:, m0 // 16 : (m0 + HALF) // 16]))
+            picked[a, h, g] = pk
+
+        def times_w4(a, t, g):
+            h, u = divmod(t, HALF // P)
+            m0 = g * S + t * P
+            for c in range(M // P):
+                nc.tensor.matmul_mx(
+                    out=acc[t][:, c * P : (c + 1) * P],
+                    lhsT=picked[a, h, g][:, u * P : (u + 1) * P].bitcast(FP8X4),
+                    lhsT_scale=planes[a][:, m0 : m0 + P],
+                    rhs=w4w[:, a, 2 * c * P : 2 * (c + 1) * P].bitcast(FP4X4),
+                    rhs_scale=w4s[:, a, c * P : (c + 1) * P],
+                    start=False,
+                    stop=False,
+                )
+
+        def times_dw(a, t, g):
+            h, u = divmod(t, HALF // P)
+            m0 = g * S + t * P
+            codes, scales = quantised[a]
+            nc.tensor.matmul_mx(
+                out=acc[t][:],
+                lhsT=picked[a, h, g][:, u * P : (u + 1) * P].bitcast(FP8X4),
+                lhsT_scale=planes[a][:, m0 : m0 + P],
+                rhs=codes[:].bitcast(FP8X4),
+                rhs_scale=scales[:],
+                start=(a == 0 and g == 0),
+                stop=(a == PASSES - 1 and g == G - 1),
+            )
+
+        slices = [(h, g) for h in range(S // HALF) for g in range(G)]
+        quantise(0)
+        for h, g in slices:
+            gather(0, h, g)
+            for t in range(2 * h, 2 * h + 2):
+                times_dw(0, t, g)
+        for t in range(TILES):
+            for g in range(G):
+                times_w4(0, t, g)
+        for h, g in slices:
+            gather(1, h, g)
+            for t in range(2 * h, 2 * h + 2):
+                times_w4(1, t, g)
+        quantise(1)
+        for t in range(TILES):
+            for g in range(G):
+                times_dw(1, t, g)
 
         for t in range(TILES):
             res = keep.tile([P, M], F32, name="res%d" % t)

@@ -35,8 +35,10 @@ def tile_list_tabbag_tm_sum_bias_kernel(tc, tab, w4_words, w4_scales, dw, b, off
         tab32 = tab.bitcast(I32)
         scale_win = keep.tile([P, T], U8, name="scale_win", align_bytes=64)
         nc.gpsimd.memset(scale_win[:].bitcast(I32), 0)
+        zero = keep.tile([P, 1], F32, name="zero")
+        nc.vector.memset(zero[:], 0.0)
         ident = keep.tile([P, P], F32, name="ident")
-        nc.vector.memset(ident[:], 0.0)
+        nc.scalar.copy(ident[:], zero[:].to_broadcast([P, P]))
         w4s = keep.tile([P, PASSES, M], U8, name="w4s", align_bytes=64)
         nc.vector.memset(w4s[:].rearrange("p a n -> p (a n)").bitcast(I32), 0)
         plane1 = keep.tile([P, G * S], U8, name="plane1", align_bytes=64)
@@ -46,17 +48,17 @@ def tile_list_tabbag_tm_sum_bias_kernel(tc, tab, w4_words, w4_scales, dw, b, off
         raw = [keep.tile([P, 4, M], F32, name="raw%d" % a) for a in range(PASSES)]
         b_col = keep.tile([P, 2], F32, name="b_col")
         nc.sync.dma_start(b_col[:], b.rearrange("(p j) -> p j", j=2))
-        nc.sync.dma_start(raw[0][:], dw[0:512, :].rearrange("(p j) n -> p j n", j=4))
+        w4w = keep.tile([P, PASSES, 2 * M], U8, name="w4w", align_bytes=64)
+        nc.sync.dma_start(w4w[:].bitcast(I32), w4_words.bitcast(I32).rearrange("a p w -> p a w"))
         rows = tab32[:, P * T :].rearrange("a (q r w) -> r q a w", q=4, r=4)
         for r in range(4):
             nc.sync.dma_start(scale_win[r:P:16, :].bitcast(I32), rows[r])
-        for a in range(PASSES):
-            nc.sync.dma_start(words[a][:].bitcast(I32), tab32[a, : P * T].rearrange("(p t) -> p t", p=P))
-        w4w = keep.tile([P, PASSES, 2 * M], U8, name="w4w", align_bytes=64)
-        nc.sync.dma_start(w4w[:].bitcast(I32), w4_words.bitcast(I32).rearrange("a p w -> p a w"))
+        nc.sync.dma_start(words[0][:].bitcast(I32), tab32[0, : P * T].rearrange("(p t) -> p t", p=P))
         w4rows = w4_scales.bitcast(I32).rearrange("a (q r) w -> r q a w", r=4)
         for r in range(4):
             nc.sync.dma_start(w4s[r:P:32, :, :].bitcast(I32), w4rows[r])
+        nc.sync.dma_start(raw[0][:], dw[0:512, :].rearrange("(p j) n -> p j n", j=4))
+        nc.sync.dma_start(words[1][:].bitcast(I32), tab32[1, : P * T].rearrange("(p t) -> p t", p=P))
         nc.sync.dma_start(raw[1][:], dw[512:1024, :].rearrange("(p j) n -> p j n", j=4))
 
         make_identity(nc, ident[:], nomemset=True)
@@ -102,7 +104,7 @@ def tile_list_tabbag_tm_sum_bias_kernel(tc, tab, w4_words, w4_scales, dw, b, off
                     lhsT_scale=planes[a][:, m0 : m0 + P],
                     rhs=w4w[:, a, 2 * c * P : 2 * (c + 1) * P].bitcast(FP4X4),
                     rhs_scale=w4s[:, a, c * P : (c + 1) * P],
-                    start=False,
+                    start=(a == 0 and g == 0 and c == 0),
                     stop=False,
                 )
 
@@ -116,27 +118,20 @@ def tile_list_tabbag_tm_sum_bias_kernel(tc, tab, w4_words, w4_scales, dw, b, off
                 lhsT_scale=planes[a][:, m0 : m0 + P],
                 rhs=codes[:].bitcast(FP8X4),
                 rhs_scale=scales[:],
-                start=(a == 0 and g == 0),
+                start=False,
                 stop=(a == PASSES - 1 and g == G - 1),
             )
 
         slices = [(h, g) for h in range(S // HALF) for g in range(G)]
-        quantise(0)
-        for h, g in slices:
-            gather(0, h, g)
-            for t in range(2 * h, 2 * h + 2):
-                times_dw(0, t, g)
-        for t in range(TILES):
-            for g in range(G):
-                times_w4(0, t, g)
-        for h, g in slices:
-            gather(1, h, g)
-            for t in range(2 * h, 2 * h + 2):
-                times_w4(1, t, g)
-        quantise(1)
-        for t in range(TILES):
-            for g in range(G):
-                times_dw(1, t, g)
+        for a in range(PASSES):
+            for h, g in slices:
+                gather(a, h, g)
+                for t in range(2 * h, 2 * h + 2):
+                    times_w4(a, t, g)
+            quantise(a)
+            for t in range(TILES):
+                for g in range(G):
+                    times_dw(a, t, g)
 
         for t in range(TILES):
             res = keep.tile([P, M], F32, name="res%d" % t)

from contextlib import ExitStack

import concourse.mybir as mybir
from concourse.masks import make_identity

G, K, M, T, S = 2, 1024, 256, 2048, 512
FLOPS = 2 * 2 * G * K * M * S

F32 = mybir.dt.float32
BF16 = mybir.dt.bfloat16
I32 = mybir.dt.int32
U32 = mybir.dt.uint32
U16 = mybir.dt.uint16
U8 = mybir.dt.uint8
FP8X4 = mybir.dt.float8_e4m3fn_x4
FP4X4 = mybir.dt.float4_e2m1fn_x4
ADD = mybir.AluOpType.add

P = 128
PASSES = K // 512
HALF = 256
TILES = S // P


def tile_list_tabbag_tm_sum_bias_kernel(tc, tab, w4_words, w4_scales, dw, b, offs, out):
    nc = tc.nc
    with ExitStack() as ctx:
        lists = ctx.enter_context(tc.tile_pool(name="lists", bufs=1))
        keep = ctx.enter_context(tc.tile_pool(name="keep", bufs=1))
        psum = ctx.enter_context(tc.psum_pool(name="psum", bufs=1))

        offsets = lists.tile([P, G * S // 16], U16, name="offsets")
        nc.sync.dma_start(offsets[:], offs)

        tab32 = tab.bitcast(I32)
        scale_win = keep.tile([P, T], U8, name="scale_win", align_bytes=64)
        nc.gpsimd.memset(scale_win[:].bitcast(I32), 0)
        zero = keep.tile([P, 1], F32, name="zero")
        nc.vector.memset(zero[:], 0.0)
        ident = keep.tile([P, P], F32, name="ident")
        nc.scalar.copy(ident[:], zero[:].to_broadcast([P, P]))
        w4s = keep.tile([P, PASSES, M], U8, name="w4s", align_bytes=64)
        nc.vector.memset(w4s[:].rearrange("p a n -> p (a n)").bitcast(I32), 0)
        plane1 = keep.tile([P, G * S], U8, name="plane1", align_bytes=64)
        nc.vector.memset(plane1[:].bitcast(I32), 0)

        words = [keep.tile([P, T], U32, name="words%d" % a, align_bytes=64) for a in range(PASSES)]
        raw = [keep.tile([P, 4, M], F32, name="raw%d" % a) for a in range(PASSES)]
        b_col = keep.tile([P, 2], F32, name="b_col")
        nc.sync.dma_start(b_col[:], b.rearrange("(p j) -> p j", j=2))
        w4w = keep.tile([P, PASSES, 2 * M], U8, name="w4w", align_bytes=64)
        nc.sync.dma_start(w4w[:].bitcast(I32), w4_words.bitcast(I32).rearrange("a p w -> p a w"))
        rows = tab32[:, P * T :].rearrange("a (q r w) -> r q a w", q=4, r=4)
        for r in range(4):
            nc.sync.dma_start(scale_win[r:P:16, :].bitcast(I32), rows[r])
        nc.sync.dma_start(words[0][:].bitcast(I32), tab32[0, : P * T].rearrange("(p t) -> p t", p=P))
        w4rows = w4_scales.bitcast(I32).rearrange("a (q r) w -> r q a w", r=4)
        for r in range(4):
            nc.sync.dma_start(w4s[r:P:32, :, :].bitcast(I32), w4rows[r])
        nc.sync.dma_start(raw[0][:], dw[0:512, :].rearrange("(p j) n -> p j n", j=4))
        nc.sync.dma_start(words[1][:].bitcast(I32), tab32[1, : P * T].rearrange("(p t) -> p t", p=P))
        nc.sync.dma_start(raw[1][:], dw[512:1024, :].rearrange("(p j) n -> p j n", j=4))

        make_identity(nc, ident[:], nomemset=True)
        bias_ps = psum.tile([P, 2, P], F32, name="bias_ps")
        for j in range(2):
            nc.tensor.transpose(bias_ps[:, j, :], b_col[:, j : j + 1].to_broadcast([P, P]), ident[:])
        bias = keep.tile([P, P, 2], F32, name="bias")
        nc.scalar.copy(bias[:], bias_ps[:].rearrange("m j p -> m p j"))

        picked_scales = keep.tile([P, G * S], U8, name="picked_scales", align_bytes=64)
        nc.vector.tensor_copy(picked_scales[:], scale_win[:].indirect(offsets[:]))
        nc.scalar.dma_start(plane1[0:100, :].bitcast(I32), picked_scales[16:116, :].bitcast(I32))
        planes = [picked_scales, plane1]

        acc = [psum.tile([P, M], F32, name="acc%d" % t) for t in range(TILES)]
        picked = {}
        quantised = {}

        def quantise(a):
            grouped = keep.tile([P, M, 4], BF16, name="grouped%d" % a, align_bytes=64)
            nc.scalar.copy(
                grouped[:].rearrange("p (c i) j -> p c j i", i=4),
                raw[a][:].rearrange("p j (c i) -> p c j i", i=4),
            )
            codes = keep.tile([P, M], U32, name="codes%d" % a, align_bytes=64)
            scales = keep.tile([P, M], U8, name="scales%d" % a, align_bytes=64)
            nc.vector.quantize_mx(out=codes[:].bitcast(FP8X4), scales=scales[:], in_=grouped[:].rearrange("p n j -> p (n j)"))
            quantised[a] = (codes, scales)

        def gather(a, h, g):
            m0 = g * S + h * HALF
            pk = keep.tile([P, HALF], U32, name="pk%d%d%d" % (a, h, g), align_bytes=64)
            nc.vector.tensor_copy(pk[:], words[a][:].indirect(offsets[:, m0 // 16 : (m0 + HALF) // 16]))
            picked[a, h, g] = pk

        def times_w4(a, t, g):
            h, u = divmod(t, HALF // P)
            m0 = g * S + t * P
            for c in range(M // P):
                nc.tensor.matmul_mx(
                    out=acc[t][:, c * P : (c + 1) * P],
                    lhsT=picked[a, h, g][:, u * P : (u + 1) * P].bitcast(FP8X4),
                    lhsT_scale=planes[a][:, m0 : m0 + P],
                    rhs=w4w[:, a, 2 * c * P : 2 * (c + 1) * P].bitcast(FP4X4),
                    rhs_scale=w4s[:, a, c * P : (c + 1) * P],
                    start=(a == 0 and g == 0 and c == 0),
                    stop=False,
                )

        def times_dw(a, t, g):
            h, u = divmod(t, HALF // P)
            m0 = g * S + t * P
            codes, scales = quantised[a]
            nc.tensor.matmul_mx(
                out=acc[t][:],
                lhsT=picked[a, h, g][:, u * P : (u + 1) * P].bitcast(FP8X4),
                lhsT_scale=planes[a][:, m0 : m0 + P],
                rhs=codes[:].bitcast(FP8X4),
                rhs_scale=scales[:],
                start=False,
                stop=(a == PASSES - 1 and g == G - 1),
            )

        slices = [(h, g) for h in range(S // HALF) for g in range(G)]
        for a in range(PASSES):
            for h, g in slices:
                gather(a, h, g)
                for t in range(2 * h, 2 * h + 2):
                    times_w4(a, t, g)
            quantise(a)
            for t in range(TILES):
                for g in range(G):
                    times_dw(a, t, g)

        for t in range(TILES):
            res = keep.tile([P, M], F32, name="res%d" % t)
            nc.vector.tensor_tensor(res[:], acc[t][:], bias[:].rearrange("m p j -> m (p j)"), ADD)
            nc.sync.dma_start(out[t * P : (t + 1) * P, :], res[:])
